import numpy as np
import ml_dtypes


def mxq(x, axis, fmt="e4m3"):
    dtype, down = {"e4m3": (ml_dtypes.float8_e4m3fn, 7), "e5m2": (ml_dtypes.float8_e5m2, 14)}[fmt]
    v = np.moveaxis(np.asarray(x, np.float32).astype(ml_dtypes.bfloat16).astype(np.float64), axis, -1)
    blocks = v.reshape(v.shape[:-1] + (-1, 32))
    amax = np.abs(blocks).max(-1, keepdims=True)
    byte = np.maximum(np.where(amax > 0, np.frexp(amax)[1] - 1 + 127, 0) - down, 1)
    scale = np.exp2(byte - 127.0)
    codes = (blocks / scale).astype(np.float32).astype(dtype).astype(np.float64)
    return np.moveaxis((codes * scale).reshape(v.shape), -1, axis)


WIDE = False


def mx_kscale(k):
    if not WIDE:
        return np.ones(k)
    levels = np.array([10, -10, 5, -5, 0])
    if k % 512:
        return np.exp2(np.random.permutation(np.resize(levels, k // 32))).repeat(32)
    a = np.empty((k // 512, 16))
    for p in range(k // 512):
        a[p, :8] = np.random.permutation(np.resize(levels, 8))
        for g in range(8):
            far = levels[np.abs(levels - a[p, g]) >= 10]
            a[p, g + 8] = far[np.random.randint(len(far))]
    return np.exp2(a.ravel()).repeat(32)


BF16 = ml_dtypes.bfloat16


def bf(x):
    return np.asarray(x, np.float32).astype(BF16)


def f64(x):
    return np.asarray(x).astype(np.float64)


E2M1 = np.array([0.0, 0.5, 1.0, 1.5, 2.0, 3.0, 4.0, 6.0, -0.0, -0.5, -1.0, -1.5, -2.0, -3.0, -4.0, -6.0])


def pack_weight(w, fmt):
    k, n = w.shape
    w = f64(bf(w)).reshape(k // 32, 32, n)
    amax = np.abs(w).max(1)
    if fmt == "e4m3":
        byte = np.frexp(amax)[1] - 1 + 127 - 7
    else:
        mant, ex = np.frexp(amax / 6.0)
        byte = np.where(mant > 0.5, ex, ex - 1) + 127
    byte = np.clip(np.where(amax > 0, byte, 1), 1, 254)
    scaled = (w * np.exp2(127.0 - byte)[:, None, :]).reshape(k, n).astype(np.float32)
    by_word = np.ascontiguousarray(scaled.reshape(k // 512, 128, 4, n).transpose(0, 1, 3, 2))
    if fmt == "e4m3":
        words = by_word.astype(ml_dtypes.float8_e4m3fn).view(np.uint8)
    else:
        c = by_word.astype(ml_dtypes.float4_e2m1fn).view(np.uint8) & 0xF
        words = c[..., 0::2] | (c[..., 1::2] << 4)
    return np.ascontiguousarray(words), np.ascontiguousarray(byte.astype(np.uint8).reshape(k // 512, 16, n))


def unpack_weight(words, scales, fmt):
    g, p, n, _ = words.shape
    if fmt == "e4m3":
        vals = np.ascontiguousarray(words).view(ml_dtypes.float8_e4m3fn).astype(np.float64)
    else:
        nib = np.empty((g, p, n, 4), np.uint8)
        nib[..., 0::2] = words & 0xF
        nib[..., 1::2] = words >> 4
        vals = E2M1[nib]
    vals = vals * np.repeat(np.exp2(scales.astype(np.float64) - 127.0), 8, axis=1)[..., None]
    return vals.transpose(0, 1, 3, 2).reshape(g * 512, n)
def pack4(w):
    words, scales = pack_weight(w, "e2m1")
    return words.reshape(words.shape[0], 128, -1), scales


def unpack4(words, scales):
    return unpack_weight(words.reshape(words.shape[0], 128, -1, 2), scales, "e2m1")


M, G, H = 1024, 2048, 512
EPS = 1e-5


def sigmoid(x):
    return 0.5 * (1.0 + np.tanh(0.5 * x))


def setup_inputs():
    s, t = mx_kscale(G), mx_kscale(H)
    size_factor = np.exp(0.4 * np.random.standard_normal(M))
    gene_rate = np.exp(0.5 * np.random.standard_normal(G))
    expected = np.random.gamma(2.0, 0.5, (M, G)) * size_factor[:, None] * gene_rate
    counts = np.random.poisson(expected).astype(np.float64)
    logged = np.log(1.0 + counts / size_factor[:, None])
    enc_words, enc_scales = pack4(np.random.standard_normal((G, H)) / np.sqrt(G) / s[:, None])
    rate_words, rate_scales = pack4(np.random.standard_normal((H, G)) / np.sqrt(H) / t[:, None])
    drop_words, drop_scales = pack4(np.random.standard_normal((H, G)) / np.sqrt(H) / t[:, None])
    return {"counts": bf(counts),
            "size_factor": bf(size_factor),
            "gene_mean": bf(logged.mean(axis=0)),
            "gene_scale": bf(s / logged.std(axis=0)),
            "enc_words": enc_words, "enc_scales": enc_scales,
            "enc_bias": bf(0.3 * np.random.standard_normal(H)),
            "lib_coef": bf(0.5 * np.random.standard_normal(H)),
            "ln_gain": bf((1.0 + 0.1 * np.random.standard_normal(H)) * t),
            "ln_bias": bf(0.2 * np.random.standard_normal(H) * t),
            "rate_words": rate_words, "rate_scales": rate_scales,
            "rate_bias": bf(0.5 * np.random.standard_normal(G)),
            "drop_words": drop_words, "drop_scales": drop_scales,
            "drop_bias": bf(0.5 * np.random.standard_normal(G)),
            "theta": bf(np.exp(0.3 * np.random.standard_normal(G)))}


def reference(counts, size_factor, gene_mean, gene_scale, enc_words, enc_scales, enc_bias, lib_coef, ln_gain, ln_bias,
              rate_words, rate_scales, rate_bias, drop_words, drop_scales, drop_bias, theta):
    sf = f64(size_factor)[:, None]
    th = f64(theta)
    x = (np.log(1.0 + f64(counts) / sf) - f64(gene_mean)) * f64(gene_scale)
    a = mxq(x, 1, "e4m3") @ unpack4(enc_words, enc_scales)
    a = a + f64(enc_bias) + np.log(sf) * f64(lib_coef)
    d = a - a.mean(axis=1, keepdims=True)
    z = d / np.sqrt((d * d).mean(axis=1, keepdims=True) + EPS)
    h = np.maximum(z * f64(ln_gain) + f64(ln_bias), 0.0)
    hq = mxq(h, 1, "e4m3")
    r = (hq @ unpack4(rate_words, rate_scales)) + f64(rate_bias)
    e = np.exp(r - r.max(axis=1, keepdims=True))
    mu = sf * G * (e / e.sum(axis=1, keepdims=True))
    pi = sigmoid((hq @ unpack4(drop_words, drop_scales)) + f64(drop_bias))
    p0 = pi + (1.0 - pi) * np.exp(-th * np.log(1.0 + mu / th))
    return mu, p0

from contextlib import ExitStack

import concourse.mybir as mybir
from concourse.masks import make_identity

M, G, H = 1024, 2048, 512
EPS = 1e-5
FLOPS = 3 * 2 * M * G * H

P = 128
PACK = 4
CELL_TILES = M // P
HALVES = 2
HALF_TILES = CELL_TILES // HALVES
HALF_CELLS = HALF_TILES * P
GROUPS = G // (P * PACK)
GENE_TILES = G // P
BANK = 512
GENE_BANKS = G // BANK

F32 = mybir.dt.float32
BF16 = mybir.dt.bfloat16
I32 = mybir.dt.int32
U32 = mybir.dt.uint32
U8 = mybir.dt.uint8
FP8X4 = mybir.dt.float8_e4m3fn_x4
FP4X4 = mybir.dt.float4_e2m1fn_x4
ALU = mybir.AluOpType
ACT = mybir.ActivationFunctionType
X = mybir.AxisListType.X


def tile_zinb_cell_autoencoder_f1_kernel(
    tc, counts, size_factor, gene_mean, gene_scale, enc_words, enc_scales, enc_bias, lib_coef,
    ln_gain, ln_bias, rate_words, rate_scales, rate_bias, drop_words, drop_scales, drop_bias, theta,
    out_0, out_1,
):
    nc = tc.nc
    counts_t = counts.rearrange("(p i) g -> i p g", i=CELL_TILES)
    mu_t = out_0.rearrange("(p i) g -> i p g", i=CELL_TILES)
    zero_t = out_1.rearrange("(p i) g -> i p g", i=CELL_TILES)

    with ExitStack() as ctx:
        const = ctx.enter_context(tc.tile_pool(name="const", bufs=1))
        rows = ctx.enter_context(tc.tile_pool(name="rows", bufs=8))
        work = ctx.enter_context(tc.tile_pool(name="work", bufs=2))
        single = ctx.enter_context(tc.tile_pool(name="single", bufs=1))
        small = ctx.enter_context(tc.tile_pool(name="small", bufs=4))
        psum = ctx.enter_context(tc.psum_pool(name="psum", bufs=4))
        ctx.enter_context(tc.manual_schedule())
        load = ctx.enter_context(tc.tile_pool(name="load", bufs=3))

        sf_b = const.tile([P, CELL_TILES], BF16, name="sf_b")
        nc.sync.dma_start(out=sf_b[:], in_=size_factor.rearrange("(p i) -> p i", i=CELL_TILES))
        gm_b = const.tile([P, GROUPS * PACK], BF16, name="gm_b")
        nc.scalar.dma_start(
            out=gm_b[:].rearrange("p (g t) -> p g t", t=PACK),
            in_=gene_mean.rearrange("(g p t) -> p g t", p=P, t=PACK),
        )
        gs_b = const.tile([P, GROUPS, PACK], BF16, name="gs_b")
        nc.scalar.dma_start(out=gs_b[:], in_=gene_scale.rearrange("(g p t) -> p g t", p=P, t=PACK))
        gain_b = const.tile([P, PACK], BF16, name="gain_b")
        nc.scalar.dma_start(out=gain_b[:], in_=ln_gain.rearrange("(p t) -> p t", t=PACK))
        lnb_b = const.tile([P, PACK], BF16, name="lnb_b")
        nc.scalar.dma_start(out=lnb_b[:], in_=ln_bias.rearrange("(p t) -> p t", t=PACK))

        cnt = {}

        def load_counts(i):
            cnt[i] = load.tile([P, G], BF16, name="cnt", tag="cnt")
            nc.sync.dma_start(out=cnt[i][:], in_=counts_t[i])

        load_counts(0)
        enc_w = const.tile([P, GROUPS * 2 * H], U8, name="enc_w", align_bytes=64)
        nc.sync.dma_start(
            out=enc_w[:].bitcast(I32).rearrange("p (g n) -> p g n", g=GROUPS),
            in_=enc_words.bitcast(I32).rearrange("g p n -> p g n"),
        )
        load_counts(1)
        enc_s = const.tile([P, GROUPS * H], U8, name="enc_s", align_bytes=64)
        nc.vector.memset(enc_s[:].bitcast(I32), 0)
        for q in range(4):
            nc.sync.dma_start(
                out=enc_s[32 * q : 32 * q + 4, :].bitcast(I32).rearrange("r (g n) -> r g n", g=GROUPS),
                in_=enc_scales.bitcast(I32).rearrange("g r n -> r g n")[4 * q : 4 * q + 4],
            )
        lib_b = const.tile([P, H], BF16, name="lib_b")
        nc.sync.dma_start(out=lib_b[:], in_=lib_coef.partition_broadcast(P))
        eb_b = const.tile([P, H], BF16, name="eb_b")
        nc.sync.dma_start(out=eb_b[:], in_=enc_bias.partition_broadcast(P))
        load_counts(2)
        stack_b = const.tile([P, P], BF16, name="stack_b")
        nc.gpsimd.memset(stack_b[:], 0.0)
        nc.sync.dma_start(out=stack_b[0:GENE_TILES, :], in_=theta.rearrange("(j p) -> j p", p=P))
        nc.sync.dma_start(out=stack_b[GENE_TILES : 2 * GENE_TILES, :], in_=drop_bias.rearrange("(j p) -> j p", p=P))
        load_counts(3)
        head_w = const.tile([P, 2, 2 * G], U8, name="head_w", align_bytes=64)
        head_s = const.tile([P, 2, G], U8, name="head_s", align_bytes=64)
        nc.gpsimd.memset(head_s[:].rearrange("p a n -> p (a n)").bitcast(I32), 0)
        for a, (words, scales) in enumerate(((drop_words, drop_scales), (rate_words, rate_scales))):
            nc.sync.dma_start(out=head_w[:, a, :].bitcast(I32), in_=words[0].bitcast(I32))
            for q in range(4):
                nc.sync.dma_start(
                    out=head_s[32 * q : 32 * q + 4, a, :].bitcast(I32),
                    in_=scales[0, 4 * q : 4 * q + 4, :].bitcast(I32),
                )
        rb_b = const.tile([P, G], BF16, name="rb_b")
        nc.sync.dma_start(out=rb_b[:], in_=rate_bias.partition_broadcast(P))
        for i in range(4, CELL_TILES):
            load_counts(i)

        one = const.tile([P, 1], F32, name="one")
        nc.vector.memset(one[:], 1.0)
        neg_half = const.tile([P, 1], F32, name="neg_half")
        nc.vector.memset(neg_half[:], -0.5)
        ident = const.tile([P, P], F32, name="ident")
        make_identity(nc, ident[:])
        rsf = const.tile([P, CELL_TILES], F32, name="rsf")
        nc.vector.reciprocal(out=rsf[:], in_=sf_b[:])
        log_sf = const.tile([P, CELL_TILES], F32, name="log_sf")
        nc.scalar.activation(out=log_sf[:], in_=sf_b[:], func=ACT.Ln)
        sf_g = const.tile([P, CELL_TILES], F32, name="sf_g")
        nc.vector.tensor_scalar_mul(sf_g[:], sf_b[:], float(G))
        select = const.tile([P, GROUPS, PACK, P], BF16, name="select")
        nc.vector.tensor_copy(
            out=select[:].rearrange("p g t n -> p (g t) n"),
            in_=ident[:, 0 : GROUPS * PACK].unsqueeze(2).to_broadcast([P, GROUPS * PACK, P]),
        )
        mean_f = const.tile([P, P], F32, name="mean_f")
        nc.gpsimd.memset(mean_f[:], 0.0)
        nc.vector.tensor_copy(out=mean_f[:, 0 : GROUPS * PACK], in_=gm_b[:])
        mean_ps = psum.tile([P, P], F32, name="mean_ps", tag="a", bufs=1)
        nc.tensor.transpose(mean_ps[:], mean_f[:], ident[:])
        neg_mean = const.tile([P, P], BF16, name="neg_mean")
        nc.vector.tensor_scalar_mul(neg_mean[:], mean_ps[:], -1.0)

        logs, x_codes, x_scales, shift, moments, rstd, z_of, acc_of, xg_of = {}, {}, {}, {}, {}, {}, {}, {}, {}
        h_codes = const.tile([P, M], U32, name="h_codes", align_bytes=64)
        h_scales = const.tile([P, M], U8, name="h_scales", align_bytes=64)

        def log_counts(i):
            logs[i] = rows.tile([P, GROUPS, PACK, P], F32, name="row", tag="row")
            src = cnt[i][:].rearrange("c (g p t) -> c g t p", g=GROUPS, t=PACK)
            for a in range(0, GROUPS, 2):
                nc.scalar.activation(
                    out=logs[i][:, a : a + 2], in_=src[:, a : a + 2], func=ACT.Ln,
                    scale=rsf[:, i : i + 1], bias=one[:],
                )

        def feature_shift(i):
            shift[i] = work.tile([P, H], F32, name="shift", tag="shift", bufs=4)
            nc.gpsimd.tensor_scalar(
                out=shift[i][:], in0=lib_b[:], scalar1=log_sf[:, i : i + 1], scalar2=0.0, op0=ALU.mult, op1=ALU.add
            )
            nc.gpsimd.tensor_tensor(out=shift[i][:], in0=shift[i][:], in1=eb_b[:], op=ALU.add)

        def standardise(i, g):
            if g == 0:
                xg_of[i] = work.tile([P, GROUPS, P, PACK], BF16, name="xg", tag="xg", align_bytes=64)
            xg = xg_of[i]
            ps = psum.tile([P, PACK, P], F32, name="ps_x", tag="x", bufs=2)
            nc.tensor.matmul(
                ps[:].rearrange("p t n -> p (t n)"), lhsT=neg_mean[:],
                rhs=select[:, g].rearrange("p t n -> p (t n)"), start=True, stop=False,
            )
            for t in range(PACK):
                nc.tensor.matmul(
                    ps[:, t, :], lhsT=logs[i][:, g, t, :], rhs=ident[:], is_transpose=True,
                    start=False, stop=(t == PACK - 1),
                )
            nc.vector.tensor_tensor(
                out=xg[:, g], in0=ps[:].rearrange("p t n -> p n t"),
                in1=gs_b[:, g, :].unsqueeze(1).to_broadcast([P, P, PACK]), op=ALU.mult,
            )

        def quantise_x(i):
            x_codes[i] = work.tile([P, GROUPS * P], U32, name="x_codes", tag="x_codes", align_bytes=64)
            x_scales[i] = work.tile([P, GROUPS * P], U8, name="x_scales", tag="x_scales", align_bytes=64)
            nc.vector.quantize_mx(
                out=x_codes[i][:].bitcast(FP8X4), scales=x_scales[i][:],
                in_=xg_of[i][:].rearrange("p g n t -> p (g n t)"),
            )

        def encode(i):
            acc_of[i] = psum.tile([P, H], F32, name="ps_a", tag="a", bufs=1)
            for g in range(GROUPS):
                cols = slice(g * P, (g + 1) * P)
                nc.tensor.matmul_mx(
                    out=acc_of[i][:], lhsT=x_codes[i][:, cols].bitcast(FP8X4), lhsT_scale=x_scales[i][:, cols],
                    rhs=enc_w[:, g * 2 * H : (g + 1) * 2 * H].bitcast(FP4X4),
                    rhs_scale=enc_s[:, g * H : (g + 1) * H],
                    start=(g == 0), stop=(g == GROUPS - 1),
                )

        def norm_statistics(i):
            a = shift[i]
            nc.vector.tensor_tensor(out=a[:], in0=acc_of[i][:], in1=a[:], op=ALU.add)
            stats = small.tile([P, 6], F32, name="stats", tag="stats")
            nc.vector.bn_stats(out=stats[:], in_=a[:])
            moments[i] = small.tile([P, 2], F32, name="moments", tag="moments")
            nc.vector.bn_aggr(out=moments[i][:], in_=stats[:])
            rstd[i] = small.tile([P, 1], F32, name="rstd", tag="rstd")
            nc.gpsimd.tensor_scalar(
                out=rstd[i][:], in0=moments[i][:, 1:2], scalar1=1.0, scalar2=EPS, op0=ALU.mult, op1=ALU.add
            )
            nc.gpsimd.tensor_tensor(out=rstd[i][:], in0=rstd[i][:], in1=neg_half[:], op=ALU.pow)

        def normalise(i):
            z_of[i] = work.tile([P, PACK, P], F32, name="z", tag="z")
            nc.vector.tensor_scalar(
                out=z_of[i][:], in0=shift[i][:].rearrange("c (m t) -> c t m", t=PACK),
                scalar1=moments[i][:, 0:1], scalar2=rstd[i][:], op0=ALU.subtract, op1=ALU.mult,
            )

        h_of, hi_of = {}, {}

        def hidden_relu(q):
            banks = [psum.tile([P, 2, 2 * P], F32, name="ps_s", tag="s", bufs=3) for half in range(2)]
            for e in range(2):
                for t in range(PACK):
                    nc.tensor.transpose(
                        banks[t // 2][:, t % 2, e * P : (e + 1) * P], z_of[2 * q + e][:, t, :], ident[:]
                    )
            h_of[q] = single.tile([P, PACK, 2 * P], BF16, name="hb", tag="hb")
            for t in range(PACK):
                nc.scalar.activation(
                    out=h_of[q][:, t, :], in_=banks[t // 2][:, t % 2, :], func=ACT.Relu,
                    scale=gain[:, t : t + 1], bias=lnb[:, t : t + 1],
                )

            hi_of[q] = single.tile([P, 2 * P, PACK], BF16, name="hi", tag="hi", align_bytes=64)
            nc.scalar.copy(out=hi_of[q][:], in_=h_of[q][:].rearrange("p t n -> p n t"))

        def hidden_quantise(q):
            hi = hi_of[q]
            cols = slice(q * 2 * P, (q + 1) * 2 * P)
            nc.vector.quantize_mx(
                out=h_codes[:, cols].bitcast(FP8X4), scales=h_scales[:, cols],
                in_=hi[:].rearrange("p n t -> p (n t)"),
            )

        rate, keep, logmu, p0, total = {}, {}, {}, {}, {}

        def keep_probability(h, j):
            if j == 0:
                keep[h] = work.tile([P, GENE_TILES, HALF_CELLS], F32, name="keep", tag="keep")
            cells = slice(h * HALF_CELLS, (h + 1) * HALF_CELLS)
            ps = psum.tile([P, HALF_CELLS], F32, name="ps_s", tag="s", bufs=3)
            nc.tensor.matmul_mx(
                out=ps[:], lhsT=head_w[:, 0, j * 2 * P : (j + 1) * 2 * P].bitcast(FP4X4),
                lhsT_scale=head_s[:, 0, j * P : (j + 1) * P],
                rhs=h_codes[:, cells].bitcast(FP8X4), rhs_scale=h_scales[:, cells], start=True, stop=True,
            )
            nc.scalar.activation(
                out=keep[h][:, j, :], in_=ps[:], func=ACT.Tanh, scale=-0.5, bias=half_bias[:, j : j + 1]
            )

        def keep_shift(h, j, engine):
            engine.tensor_scalar(
                out=keep[h][:, j, :], in0=keep[h][:, j, :], scalar1=0.5, scalar2=0.5, op0=ALU.mult, op1=ALU.add
            )

        def rate_logits(i, b):
            if b == 0:
                rate[i] = rows.tile([P, G], F32, name="row", tag="row")
            cells = slice(i * P, (i + 1) * P)
            genes = slice(b * BANK, (b + 1) * BANK)
            ps = psum.tile([P, BANK], F32, name="ps_r", tag="r", bufs=2)
            nc.tensor.matmul_mx(
                out=ps[:], lhsT=h_codes[:, cells].bitcast(FP8X4), lhsT_scale=h_scales[:, cells],
                rhs=head_w[:, 1, b * 2 * BANK : (b + 1) * 2 * BANK].bitcast(FP4X4),
                rhs_scale=head_s[:, 1, genes], start=True, stop=True,
            )
            nc.vector.tensor_tensor(out=rate[i][:, genes], in0=ps[:], in1=rb_b[:, genes], op=ALU.add)

        neg_max = {}

        def row_max(i):
            neg_max[i] = small.tile([P, 1], F32, name="neg_max", tag="neg_max")
            nc.vector.tensor_reduce(out=neg_max[i][:], in_=rate[i][:], axis=X, op=ALU.max, negate=True)

        def exponential(i):
            total[i] = small.tile([P, 1], F32, name="total", tag="total")
            nc.scalar.activation(
                out=rate[i][:], in_=rate[i][:], func=ACT.Exp, bias=neg_max[i][:], accum_out=total[i][:]
            )

        def scale_mu(i):
            factor = small.tile([P, 1], F32, name="factor", tag="factor")
            nc.vector.reciprocal(out=factor[:], in_=total[i][:])
            nc.gpsimd.tensor_scalar(
                out=rate[i][:], in0=rate[i][:], scalar1=factor[:], scalar2=sf_g[:, i : i + 1],
                op0=ALU.mult, op1=ALU.mult,
            )
            nc.sync.dma_start(out=mu_t[i], in_=rate[i][:])

        def log_mu(h, j):
            if j == 0:
                logmu[h] = single.tile([P, GENE_TILES, HALF_CELLS], F32, name="logmu", tag="logmu")
            ps = psum.tile([P, HALF_TILES, P], F32, name="ps_s", tag="s", bufs=3)
            for e in range(HALF_TILES):
                nc.tensor.transpose(ps[:, e, :], rate[h * HALF_TILES + e][:, j * P : (j + 1) * P], ident[:])
            nc.scalar.activation(
                out=logmu[h][:, j, :], in_=ps[:].rearrange("p e n -> p (e n)"), func=ACT.Ln,
                scale=rtheta[:, j : j + 1], bias=one[:],
            )
            engine = nc.vector if h == 1 and j % 2 == 1 else nc.gpsimd
            engine.tensor_scalar(
                out=logmu[h][:, j, :], in0=logmu[h][:, j, :], scalar1=th[:, j : j + 1], scalar2=0.0,
                op0=ALU.mult, op1=ALU.add,
            )

        def turned(src, e, b, tag, bufs):
            ps = psum.tile([P, 4, P], F32, name="ps_" + tag, tag=tag, bufs=bufs)
            for k in range(4):
                nc.tensor.transpose(ps[:, k, :], src[:, 4 * b + k, e * P : (e + 1) * P], ident[:])
            return ps[:].rearrange("p k n -> p (k n)")

        def zero_power(h, e, b):
            i = h * HALF_TILES + e
            if b == 0:
                p0[i] = rows.tile([P, G], F32, name="row", tag="row")
            nc.scalar.activation(
                out=p0[i][:, b * BANK : (b + 1) * BANK], in_=turned(logmu[h], e, b, "s", 3), func=ACT.Exp, scale=-1.0
            )

        def zero_product(h, e, b):
            i = h * HALF_TILES + e
            genes = slice(b * BANK, (b + 1) * BANK)
            nc.vector.scalar_tensor_tensor(
                out=p0[i][:, genes], in0=p0[i][:, genes], scalar=1.0, in1=turned(keep[h], e, b, "r", 2),
                op0=ALU.subtract, op1=ALU.mult,
            )

        def store_zero(i, engine, parts):
            width = G // parts
            for k in range(parts):
                genes = slice(k * width, (k + 1) * width)
                engine.tensor_scalar(
                    out=p0[i][:, genes], in0=p0[i][:, genes], scalar1=1.0, scalar2=1.0, op0=ALU.mult, op1=ALU.add
                )
                nc.sync.dma_start(out=zero_t[i][:, genes], in_=p0[i][:, genes])

        def encoder_half(h, beside):
            t0 = h * HALF_TILES
            for e in range(HALF_TILES):
                for g in range(GROUPS):
                    standardise(t0 + e, g)
                    if g == 0 and e >= 2:
                        normalise(t0 + e - 2)
                        if h == 0:
                            feature_shift(t0 + e + 2)
                    if g == 1 and e >= 1:
                        encode(t0 + e - 1)
                    if g == 2 and e == 3:
                        hidden_relu(2 * h)
                    beside(GROUPS * e + g)
                quantise_x(t0 + e)
                if e >= 1:
                    norm_statistics(t0 + e - 1)
            hidden_quantise(2 * h)
            encode(t0 + 3)
            beside(16)
            rate_logits(t0, 0)
            rate_logits(t0, 1)
            norm_statistics(t0 + 3)
            normalise(t0 + 2)
            beside(17)
            rate_logits(t0, 2)
            rate_logits(t0, 3)
            normalise(t0 + 3)
            beside(18)
            hidden_relu(2 * h + 1)
            row_max(t0)
            hidden_quantise(2 * h + 1)
            if h == 0:
                feature_shift(6)
                feature_shift(7)

        def rate_half(h, shifts):
            t0 = h * HALF_TILES
            exponential(t0)
            for e in range(1, HALF_TILES):
                for b in range(GENE_BANKS):
                    rate_logits(t0 + e, b)
                    keep_probability(h, 4 * (e - 1) + b)
                scale_mu(t0 + e - 1)
                for k in range(shifts):
                    keep_shift(h, shifts * (e - 1) + k, nc.gpsimd)
                row_max(t0 + e)
                exponential(t0 + e)

        for i in range(4):
            feature_shift(i)
        for i in range(4):
            log_counts(i)
        gain = const.tile([P, PACK], F32, name="gain")
        lnb = const.tile([P, PACK], F32, name="lnb")

        def more_logs(step):
            if step in (4, 8):
                log_counts(3 + step // 4)
            if step == 4:
                nc.vector.tensor_copy(out=gain[:], in_=gain_b[:])
                nc.vector.tensor_copy(out=lnb[:], in_=lnb_b[:])
            if step == 15:
                log_counts(6)
                log_counts(7)

        encoder_half(0, more_logs)

        stack_f = const.tile([P, P], F32, name="stack_f")
        nc.vector.tensor_copy(out=stack_f[:], in_=stack_b[:])
        stack_ps = psum.tile([P, P], F32, name="stack_ps", tag="a", bufs=1)
        nc.tensor.transpose(stack_ps[:], stack_f[:], ident[:])
        th = const.tile([P, GENE_TILES], F32, name="th")
        nc.vector.tensor_copy(out=th[:], in_=stack_ps[:, 0:GENE_TILES])
        half_bias = const.tile([P, GENE_TILES], F32, name="half_bias")
        nc.vector.tensor_scalar_mul(half_bias[:], stack_ps[:, GENE_TILES : 2 * GENE_TILES], -0.5)
        rtheta = const.tile([P, GENE_TILES], F32, name="rtheta")
        nc.vector.reciprocal(out=rtheta[:], in_=th[:])

        rate_half(0, 2)

        def jobs_of(h):
            return [(log_mu, (h, j)) for j in range(GENE_TILES)]

        def powers_of(h):
            return [(zero_power, (h, e, b)) for e in range(HALF_TILES) for b in range(GENE_BANKS)]

        def run(queue, first, last):
            for fn, args in queue[max(first, 0) : max(last, 0)]:
                fn(*args)

        jobs_a = jobs_of(0) + powers_of(0)
        late_a = [(keep_shift, (0, j, nc.gpsimd)) for j in range(3 * 2, GENE_TILES)]

        def decoder_beside(step):
            if step < GENE_BANKS:
                keep_probability(0, 12 + step)
            if step == 1:
                scale_mu(3)
            run(jobs_a, 2 * (step - 4), 2 * (step - 4 + 1))
            run(late_a, 2 * (step - 12), 2 * (step - 11))

        encoder_half(1, decoder_beside)
        run(jobs_a, 2 * (19 - 4), len(jobs_a))
        run(late_a, 14, len(late_a))
        rate_half(1, 3)
        jobs_b = jobs_of(1)
        late_b = [(keep_shift, (1, j, nc.vector)) for j in range(3 * 3, GENE_TILES)]
        for k in range(GENE_TILES):
            zero_product(0, k // 4, k % 4)
            if k < GENE_BANKS:
                keep_probability(1, 12 + k)
            if k == 3:
                scale_mu(7)
            run(jobs_b, 2 * (k - 8), 2 * (k - 8 + 1))
            run(late_b, 2 * (k - 12), 2 * (k - 11))
            if k % 4 == 3:
                store_zero(k // 4, nc.vector, 1)
        run(jobs_b, 2 * (GENE_TILES - 8), len(jobs_b))
        run(late_b, 8, len(late_b))
        for k in range(GENE_TILES + 2):
            if k < GENE_TILES:
                zero_power(1, k // 4, k % 4)
            if k >= 2:
                zero_product(1, (k - 2) // 4, (k - 2) % 4)
                if k % 4 == 1:
                    i = 4 + (k - 2) // 4
                    store_zero(i, nc.gpsimd if i < 7 else nc.vector, 1 if i < 7 else 4)
